import numpy as np
import ml_dtypes


def mxq(x, axis, fmt="e4m3"):
    dtype, down = {"e4m3": (ml_dtypes.float8_e4m3fn, 7), "e5m2": (ml_dtypes.float8_e5m2, 14)}[fmt]
    v = np.moveaxis(np.asarray(x, np.float32).astype(ml_dtypes.bfloat16).astype(np.float64), axis, -1)
    blocks = v.reshape(v.shape[:-1] + (-1, 32))
    amax = np.abs(blocks).max(-1, keepdims=True)
    byte = np.maximum(np.where(amax > 0, np.frexp(amax)[1] - 1 + 127, 0) - down, 1)
    scale = np.exp2(byte - 127.0)
    codes = (blocks / scale).astype(np.float32).astype(dtype).astype(np.float64)
    return np.moveaxis((codes * scale).reshape(v.shape), -1, axis)


WIDE = False


def mx_kscale(k):
    if not WIDE:
        return np.ones(k)
    levels = np.array([10, -10, 5, -5, 0])
    if k % 512:
        return np.exp2(np.random.permutation(np.resize(levels, k // 32))).repeat(32)
    a = np.empty((k // 512, 16))
    for p in range(k // 512):
        a[p, :8] = np.random.permutation(np.resize(levels, 8))
        for g in range(8):
            far = levels[np.abs(levels - a[p, g]) >= 10]
            a[p, g + 8] = far[np.random.randint(len(far))]
    return np.exp2(a.ravel()).repeat(32)


BF16 = ml_dtypes.bfloat16


def bf(x):
    return np.asarray(x, np.float32).astype(BF16)


def f64(x):
    return np.asarray(x).astype(np.float64)

def planes(Y):
    n, m = Y.shape
    b = f64(bf(Y)).reshape(n // 32, 32, m)
    amax = np.abs(b).max(1)
    byte = np.clip(np.where(amax > 0, np.frexp(amax)[1] - 1 + 127 - 7, 1), 1, 254)
    codes = (b * np.exp2(127.0 - byte)[:, None, :]).reshape(n, m).astype(np.float32).astype(ml_dtypes.float8_e4m3fn).view(np.uint8)
    words = codes.reshape(n // 512, 128, 4, m).transpose(0, 1, 3, 2)
    return np.ascontiguousarray(words), np.ascontiguousarray(byte.astype(np.uint8).reshape(n // 512, 16, m))


S, N, P, M = 1024, 1024, 1024, 1024

TAIL_WIDTH = 0.25


def setup_inputs():
    s = mx_kscale(N)
    t = mx_kscale(S)
    r = bf(np.random.standard_normal((S, N)) * s)
    h = bf(np.random.standard_normal((N, P)) / np.sqrt(N) / s[:, None])
    v = bf(np.random.uniform(0.4, 1.2, P))
    vr = bf((1.0 + 0.1 * np.random.standard_normal(S)) * t)
    y = bf(np.random.standard_normal((S, M)) / t[:, None])
    return {"r": r, "h": h, "v": v, "vr": vr, "y": y}


def smooth_tail_indicator(losses, thresholds):
    return 1.0 / (1.0 + np.exp(-(losses - thresholds[None, :]) / TAIL_WIDTH))


def relative_tail_weight(w):
    return w / np.mean(w, axis=0, keepdims=True) - 1.0


def core(r, h, v, vr, y):
    num_scenarios = r.shape[0]
    l = mxq(f64(r), 1, "e4m3") @ mxq(f64(h), 0, "e4m3")
    w = smooth_tail_indicator(l, f64(v))
    c = relative_tail_weight(w)
    e = c * f64(vr)[:, None]
    return (mxq(e, 0, "e4m3").T @ mxq(f64(y), 0, "e4m3")) / np.sqrt(num_scenarios)


def reference(r, h, v, vr, y):
    R_out = core(r, h, v, vr, y)
    words, scales = planes(R_out)
    return R_out, words, scales

from contextlib import ExitStack

import concourse.mybir as mybir
from concourse.masks import make_identity

F32 = mybir.dt.float32
BF16 = mybir.dt.bfloat16
U32 = mybir.dt.uint32
I32 = mybir.dt.int32
U8 = mybir.dt.uint8
FP8X4 = mybir.dt.float8_e4m3fn_x4
ACT = mybir.ActivationFunctionType
ALU = mybir.AluOpType

P = 128
SIZE = 1024
FLOPS = 2 * 2 * SIZE * SIZE * SIZE

ORDER = (
    "LR02+q LH10q RT02p RT03p LR00+q RE03s RE02v HI010+v LH00q RT00p RE00s LR13q LR11q RT01p HQ010v LR12q "
    "LR10q RQ011v HI000s RT13p HI001v RQ001v RE13s RT11p RE01v LH11q RT12p HQ000v RT10p RQ000v RE11s RE12s "
    "RE10s LH01q HI110s RQ010v HQ011v M110p HQ001v RQ101v HI111v RQ100v M100p HI101s RQ110v RQ111v HI100v M120p "
    "SG20s M101p M131p HQ110+v M111p M121p HQ100+v LY0q SG00s YI00v LY1q YI02+v M171p SG31s SG01s M160p "
    "M141p M150p SG21s M130p SG10s AD0v M170p YI12+v M140p RC0v AD2s RC2v SG11s SG71s YQ00v CC21v "
    "YI11v M161p CC00+v SG30s CT21p SG70s CT00p YQ02+v AD1s SG40s AD7v RC1v CC20g CT01p AD3v EE21v "
    "CC10g RC3v EE00v EE01v SG41s YI10s RC7v M151p CT20p AD4v EE20v CC11s CC30+g CT10p RC4v YQ12+v "
    "CT30p SG61s YI01s EQ0v SG60s SG50s CC40g EQ2v CT11p CT31p SG51s YQ10+v M221p M201p YQ01v EE31v "
    "CC70g AD6v EE10v OE01s EE30v RC6v CC41g AD5s M200p M220p CT70p CC71s CT40p OE20s OE21s CC60s "
    "EE11v CT41p EQ3v CT71p RC5v EQ1v CC51g CC61g SO01q M230p EE40v OE00s M210p M231p M211p OE30s "
    "CC50g CT60p CT51p OE10s EE70v EE41v OE31s EE71v EQ4v CT61p EQ7v OI00v CT50p OE11s M271p EE60v "
    "OI01s EE51v SO20q EE61v SO21q M240p SO30q SO00q OQ01v OE71s SO31q EE50v OE40s M270p EQ6v M241p "
    "EQ5v OE70s M261p SO11q M251p OE41s OI02+v SO10q SW01q SO71q OE61s M260p OQ00v OE51s OQ02+v OE60s "
    "SO40q SO70q SO41q M250p OE50s OI12+v SO61q OI10v OQ12+v OI11s SO51q SS0q OQ10+v SO60q SW02+q SO50q "
    "SW12+q SW10+q SS1q SW00q "
).split()


def tile_smoothedtailfilteredreversestress_x1_kernel(tc, r, h, v, vr, y, out_0, out_1, out_2):
    nc = tc.nc
    with ExitStack() as ctx:
        sb = ctx.enter_context(tc.tile_pool(name="sb", bufs=1))
        psum = ctx.enter_context(tc.psum_pool(name="psum", bufs=1))
        ctx.enter_context(tc.manual_schedule())
        tiles = {}

        def tile(key, shape, dtype, tag=None):
            if key not in tiles:
                tiles[key] = sb.tile(shape, dtype, name=key, tag=tag or key, align_bytes=64)
            return tiles[key]

        free_banks = list(range(8))
        open_banks = {}

        def take_bank(key):
            b = free_banks.pop(0)
            open_banks[key] = (b, psum.tile([P, 512], F32, name="ps_" + key, tag="bank%d" % b))
            return open_banks[key][1]

        def empty_bank(key):
            b, bank = open_banks[key]
            free_banks.append(b)
            return bank

        def copy(eng, out, in_):
            if eng == "v":
                nc.vector.tensor_copy(out=out, in_=in_)
            else:
                nc.scalar.copy(out=out, in_=in_)

        def codes(name, width):
            return tile(name + "_codes", [P, width], U32), tile(name + "_scales", [P, width], U8)

        def quantize(name, width, first, in_):
            c, s = codes(name, width)
            n = in_.shape[1] // 4
            nc.vector.quantize_mx(out=c[:, first : first + n].bitcast(FP8X4), scales=s[:, first : first + n], in_=in_)

        def mx_pair(bank, lhs, lhs_first, rhs, rhs_first):
            for k in range(2):
                lc, ls = lhs[k]
                rc, rs = rhs[k]
                a, b = lhs_first[k], rhs_first[k]
                nc.tensor.matmul_mx(
                    out=bank[:],
                    lhsT=lc[:, a : a + P].bitcast(FP8X4),
                    lhsT_scale=ls[:, a : a + P],
                    rhs=rc[:, b : b + 512].bitcast(FP8X4),
                    rhs_scale=rs[:, b : b + 512],
                    start=(k == 0),
                    stop=(k == 1),
                )

        warm = tile("warm", [P, 16], F32)
        nc.vector.memset(warm[:, 0:1], 0.0)
        nc.scalar.activation(out=warm[:, 8:9], in_=warm[:, 0:1], func=ACT.Sigmoid)
        ident = tile("ident", [P, P], F32)
        make_identity(nc, ident[:])
        v_raw = tile("v_raw", [P, 2, 16], BF16)
        vr_raw = tile("vr_raw", [P, 2, 16], BF16)
        nc.gpsimd.dma_start(out=v_raw[:, :, 0:4], in_=v.rearrange("(g q t) -> q g t", g=2, t=4))
        nc.gpsimd.dma_start(out=vr_raw[:, :, 0:4], in_=vr.rearrange("(g q t) -> q g t", g=2, t=4))
        bias = tile("bias", [P, 2, 4], F32)
        gain = tile("gain", [P, 2, 4], F32)
        nc.gpsimd.tensor_scalar(out=bias[:], in0=v_raw[:, :, 0:4], scalar1=-4.0, scalar2=0.0, op0=ALU.mult, op1=ALU.add)
        nc.gpsimd.tensor_scalar(out=gain[:], in0=vr_raw[:, :, 0:4], scalar1=float(SIZE), scalar2=0.0, op0=ALU.mult, op1=ALU.add)

        r_rows = r.rearrange("(s q t) k -> s q t k", s=2, t=4)
        h_rows = h.rearrange("(k q j) c -> k q j c", k=2, j=4)
        y_rows = y.rearrange("(s q j) m -> s q j m", s=2, j=4)
        out_rows = out_0.rearrange("(g q t) m -> g t q m", g=2, t=4)

        def r_raw(s):
            return tile("r_raw%d" % s, [P, 4, SIZE], BF16)

        def r_words(s, tp):
            return tile("r_words%d%d" % (s, tp), [P, 2, 2, P, 2], F32)

        def h_raw(k, g):
            return tile("h_raw%d%d" % (k, g), [P, 4, 512], BF16)

        def h_bf(g, k):
            return tile("h_bf%d%d" % (g, k), [P, 4, P, 4], BF16)

        def y_raw(s):
            return tile("y_raw%d" % s, [P, 4, SIZE], BF16)

        def y_bf(s):
            return tile("y_bf%d" % s, [P, SIZE, 4], BF16)

        def w(i):
            return tile("w%d" % i, [P, SIZE], F32)

        half_sums = tile("half_sums", [P, 8, 2], F32)
        sums = tile("sums", [P, 8], F32)
        inverse = tile("inverse", [P, 8], F32)

        def e_bf(pair):
            return tile("e_bf%d" % pair, [P, 2, 2, P, 4], BF16, tag="r_words%d%d" % divmod(pair, 2))

        def o32(g, half):
            return tile("o32_%d%d" % (g, half), [P, 4, 512], F32)

        def o_bf(g, half):
            return tile("o_bf%d%d" % (g, half), [P, 512, 4], BF16, tag="h_bf%d%d" % (g, half))

        def interleave(eng, out, in_):
            if eng == "g":
                nc.gpsimd.tensor_scalar(out=out, in0=in_.rearrange("p j m -> p m j"), scalar1=1.0, scalar2=-0.0, op0=ALU.mult, op1=ALU.add)
            else:
                copy(eng, out.rearrange("p (c i) j -> p c j i", i=4), in_.rearrange("p j (c i) -> p c j i", i=4))

        for step in ORDER:
            kind, eng = step[0:2], step[-1]
            count = 2 if step[-2] == "+" else 1
            key = step[2 : len(step) - count]
            a = [int(ch) for ch in key]
            first, last = a[-1], a[-1] + count
            if kind == "LH":
                nc.sync.dma_start(out=h_raw(*a)[:], in_=h_rows[a[0]][:, :, 512 * first : 512 * last])
            elif kind == "LR":
                nc.sync.dma_start(out=r_raw(a[0])[:, first:last], in_=r_rows[a[0]][:, first:last])
            elif kind == "LY":
                nc.sync.dma_start(out=y_raw(a[0])[:], in_=y_rows[a[0]])
            elif kind == "HI":
                g, k, half = a
                ms = slice(64 * first, 64 * last)
                copy(eng, h_bf(g, k)[:].rearrange("p t m j -> p m j t")[:, ms], h_raw(k, g)[:].rearrange("p j (m t) -> p m j t", t=4)[:, ms])
            elif kind == "HQ":
                g, k, tp = a
                quantize("h%d%d" % (g, k), 512, 256 * first, h_bf(g, k)[:, 2 * first : 2 * last].rearrange("p t m j -> p (t m j)"))
            elif kind == "RT":
                bank = take_bank("r" + key)
                words = r_raw(a[0])[:, a[1]].bitcast(F32)
                for k in range(2):
                    for u in range(2):
                        n = 2 * k + u
                        nc.tensor.transpose(bank[:, P * n : P * (n + 1)], words[:, 256 * k + u : 256 * (k + 1) : 2], ident[:])
            elif kind == "RE":
                s, t = a
                bank = empty_bank("r" + key)
                copy(eng, r_words(s, t // 2)[:, :, t % 2], bank[:].rearrange("p (k u q) -> p k q u", k=2, u=2))
            elif kind == "RQ":
                s, k, tp = a
                quantize("r%d%d" % (s, k), 512, 256 * first, r_words(s, tp)[:, k].rearrange("p t q u -> p (t q u)").bitcast(BF16))
            elif kind == "M1":
                i, s = a
                bank = take_bank("l" + key)
                mx_pair(bank, [codes("h%d%d" % (i // 4, k), 512) for k in range(2)], [P * (i % 4)] * 2,
                        [codes("r%d%d" % (s, k), 512) for k in range(2)], [0, 0])
            elif kind == "SG":
                i, s = a
                bank = empty_bank("l" + key)
                nc.scalar.activation(out=w(i)[:, 512 * s : 512 * (s + 1)], in_=bank[:], func=ACT.Sigmoid,
                                     bias=bias[:, i // 4, i % 4 : i % 4 + 1], scale=4.0, accum_out=half_sums[:, i, s : s + 1])
            elif kind == "AD":
                i = a[0]
                if eng == "s":
                    nc.scalar.activation(out=sums[:, i : i + 1], in_=half_sums[:, i, 0:1], func=ACT.Identity, bias=half_sums[:, i, 1:2], scale=1.0)
                else:
                    nc.vector.tensor_reduce(out=sums[:, first:last], in_=half_sums[:, first:last, :], axis=mybir.AxisListType.X, op=ALU.add)
            elif kind == "RC":
                nc.vector.reciprocal(out=inverse[:, first:last], in_=sums[:, first:last])
            elif kind == "CC":
                i, s = a
                half = w(i)[:, 512 * first : 512 * last]
                if eng == "s":
                    nc.scalar.activation(out=half, in_=half, func=ACT.Copy, bias=-1.0 / SIZE, scale=inverse[:, i : i + 1])
                else:
                    engine = nc.vector if eng == "v" else nc.gpsimd
                    engine.tensor_scalar(out=half, in0=half, scalar1=inverse[:, i : i + 1], scalar2=-1.0 / SIZE, op0=ALU.mult, op1=ALU.add)
            elif kind == "CT":
                i, s = a
                bank = take_bank("c" + key)
                for t in range(4):
                    nc.tensor.transpose(bank[:, P * t : P * (t + 1)], w(i)[:, 512 * s + P * t : 512 * s + P * (t + 1)], ident[:])
            elif kind == "EE":
                i, s = a
                bank = empty_bank("c" + key)
                nc.vector.tensor_tensor(out=e_bf(i // 2)[:, i % 2, s], in0=bank[:].rearrange("q (t p) -> q p t", t=4),
                                        in1=gain[:, s, :].unsqueeze(1).to_broadcast([P, P, 4]), op=ALU.mult)
            elif kind == "EQ":
                g, t = divmod(first, 4)
                quantize("e%d" % g, SIZE, 256 * t, e_bf(first // 2)[:, t % 2 : t % 2 + count].rearrange("q i s p t -> q (i s p t)"))
            elif kind == "YI":
                s, q = a
                interleave(eng, y_bf(s)[:, 256 * first : 256 * last], y_raw(s)[:, :, 256 * first : 256 * last])
            elif kind == "YQ":
                s, q = a
                quantize("y%d" % s, SIZE, 256 * q, y_bf(s)[:, 256 * first : 256 * last].rearrange("p m j -> p (m j)"))
            elif kind == "M2":
                i, half = a
                bank = take_bank("o" + key)
                mx_pair(bank, [codes("e%d" % (i // 4), SIZE)] * 2, [256 * (i % 4), 256 * (i % 4) + P], [codes("y%d" % s, SIZE) for s in range(2)], [512 * half] * 2)
            elif kind == "OE":
                i, half = a
                bank = empty_bank("o" + key)
                dst = o32(i // 4, half)[:, i % 4]
                if eng == "s":
                    nc.scalar.activation(out=dst, in_=bank[:], func=ACT.Copy, scale=1.0 / 32.0)
                else:
                    nc.vector.tensor_scalar(out=dst, in0=bank[:], scalar1=1.0 / 32.0, scalar2=None, op0=ALU.mult)
            elif kind == "SO":
                i, half = a
                cols = slice(512 * first, 512 * last)
                nc.sync.dma_start(out=out_rows[i // 4, i % 4][:, cols], in_=o32(i // 4, half)[:, i % 4])
            elif kind == "OI":
                g, q = a
                interleave(eng, o_bf(g, q // 2)[:, 256 * (q % 2) : 256 * (q % 2 + count)], o32(g, q // 2)[:, :, 256 * (q % 2) : 256 * (q % 2 + count)])
            elif kind == "OQ":
                g, q = a
                quantize("o%d" % g, SIZE, 256 * q, o_bf(g, q // 2)[:, 256 * (q % 2) : 256 * (q % 2 + count)].rearrange("p m t -> p (m t)"))
            elif kind == "SW":
                g, q = a
                cols = slice(256 * first, 256 * last)
                nc.sync.dma_start(out=out_1[g].rearrange("p m t -> p (m t)").bitcast(I32)[:, cols],
                                  in_=codes("o%d" % g, SIZE)[0][:].bitcast(I32)[:, cols])
            else:
                g = a[0]
                for quad in range(4):
                    nc.sync.dma_start(out=out_2[g, 4 * quad : 4 * quad + 4, :].bitcast(I32),
                                      in_=codes("o%d" % g, SIZE)[1][32 * quad : 32 * quad + 4, :].bitcast(I32))
